import numpy as np
import ml_dtypes


def mxq(x, axis, fmt="e4m3"):
    dtype, down = {"e4m3": (ml_dtypes.float8_e4m3fn, 7), "e5m2": (ml_dtypes.float8_e5m2, 14)}[fmt]
    v = np.moveaxis(np.asarray(x, np.float32).astype(ml_dtypes.bfloat16).astype(np.float64), axis, -1)
    blocks = v.reshape(v.shape[:-1] + (-1, 32))
    amax = np.abs(blocks).max(-1, keepdims=True)
    byte = np.maximum(np.where(amax > 0, np.frexp(amax)[1] - 1 + 127, 0) - down, 1)
    scale = np.exp2(byte - 127.0)
    codes = (blocks / scale).astype(np.float32).astype(dtype).astype(np.float64)
    return np.moveaxis((codes * scale).reshape(v.shape), -1, axis)


WIDE = False


def mx_kscale(k):
    if not WIDE:
        return np.ones(k)
    levels = np.array([10, -10, 5, -5, 0])
    if k % 512:
        return np.exp2(np.random.permutation(np.resize(levels, k // 32))).repeat(32)
    a = np.empty((k // 512, 16))
    for p in range(k // 512):
        a[p, :8] = np.random.permutation(np.resize(levels, 8))
        for g in range(8):
            far = levels[np.abs(levels - a[p, g]) >= 10]
            a[p, g + 8] = far[np.random.randint(len(far))]
    return np.exp2(a.ravel()).repeat(32)


def f64(x):
    return np.asarray(x).astype(np.float64)


def striped(idx):
    return np.tile(idx.reshape(-1, 16).T, (8, 1)).astype(np.uint16)


def unstriped(offs):
    return offs[:16].T.reshape(-1).astype(np.int64)


def pack_weight(w):
    k, n = w.shape
    w = f64(np.asarray(w, np.float32).astype(ml_dtypes.bfloat16)).reshape(k // 32, 32, n)
    amax = np.abs(w).max(1)
    byte = np.clip(np.where(amax > 0, np.frexp(amax)[1] - 1 + 127 - 7, 1), 1, 254)
    scaled = (w * np.exp2(127.0 - byte)[:, None, :]).reshape(k, n).astype(np.float32)
    words = np.ascontiguousarray(scaled.reshape(k // 512, 128, 4, n).transpose(0, 1, 3, 2)).astype(ml_dtypes.float8_e4m3fn).view(np.uint8)
    return words, np.ascontiguousarray(byte.astype(np.uint8).reshape(k // 512, 16, n))


def unpack_weight(words, scales):
    g, p, n, _ = words.shape
    vals = np.ascontiguousarray(words).view(ml_dtypes.float8_e4m3fn).astype(np.float64) * np.repeat(np.exp2(scales.astype(np.float64) - 127.0), 8, axis=1)[..., None]
    return vals.transpose(0, 1, 3, 2).reshape(g * 512, n)


K, T, S, N, H, U = 1024, 1024, 512, 128, 512, 1024


def setup_inputs():
    n = np.random.standard_normal
    s = mx_kscale(K)[:, None]
    u = mx_kscale(H)
    packed_xT = pack_weight(n((K, T)) * s)
    return {
        "x_words": packed_xT[0],
        "x_scales": packed_xT[1],
        "w1": (n((K, H)) / np.sqrt(K) / s).astype(np.float32),
        "w2": (n((K, H)) / np.sqrt(K) / s).astype(np.float32),
        "unit": (np.random.uniform(0.6, 1.4, (H, 1)) * u[:, None]).astype(np.float32),
        "w3": (n((H, N)) / np.sqrt(H) / u[:, None]).astype(np.float32),
        "offs": striped(np.random.permutation(T)[:S]),
        "up_": striped(np.random.permutation(np.concatenate([np.arange(S), np.random.randint(0, S, U - S)]))),
        "dn": striped(np.random.permutation(np.concatenate([np.arange(S), np.random.randint(0, S, U - S)]))),
    }


def reference(x_words, x_scales, w1, w2, unit, w3, offs, up_, dn):
    xq = unpack_weight(x_words, x_scales)[:, unstriped(offs)]
    y = mxq(f64(w1), 0, "e4m3").T @ xq
    yu = y[:, unstriped(up_)]
    yd_ = y[:, unstriped(dn)]
    head = yu - yd_
    z1 = mxq(f64(w2), 0, "e4m3").T @ xq
    zu = z1[:, unstriped(up_)]
    hid = f64(unit) * (head * np.abs(zu))
    return mxq(f64(w3), 0, "e4m3").T @ mxq(hid, 0, "e4m3")

@@ -1,0 +1,170 @@
+from contextlib import ExitStack
+
+import concourse.mybir as mybir
+
+K, T, S, N, H, U = 1024, 1024, 512, 128, 512, 1024
+FLOPS = 2 * (2 * K * H * S + H * N * U)
+
+F32 = mybir.dt.float32
+BF16 = mybir.dt.bfloat16
+I32 = mybir.dt.int32
+U32 = mybir.dt.uint32
+U16 = mybir.dt.uint16
+U8 = mybir.dt.uint8
+FP8X4 = mybir.dt.float8_e4m3fn_x4
+ALU = mybir.AluOpType
+ACT = mybir.ActivationFunctionType
+
+P = 128
+PACK = 4
+K_PASS = P * PACK
+PASSES = K // K_PASS
+STRIPE = 16
+SPARE = 16
+Y_WIDTH = U + SPARE
+CHUNKS = (512, 256, 128, 128)
+
+
+def tile_picked_yflowsq_lin_p_kernel(
+    tc, x_words, x_scales, w1, w2, unit, w3, offs, up_, dn, out
+):
+    nc = tc.nc
+    with ExitStack() as ctx:
+        keep = ctx.enter_context(tc.tile_pool(name="keep", bufs=1))
+        psum = ctx.enter_context(tc.psum_pool(name="psum", bufs=1))
+
+        offs_t = keep.tile([P, S // STRIPE], U16, name="offs_t")
+        up_t = keep.tile([P, U // STRIPE], U16, name="up_t")
+        dn_t = keep.tile([P, U // STRIPE], U16, name="dn_t")
+        unit_t = keep.tile([P, PACK], F32, name="unit_t")
+        xw = [keep.tile([P, T], U32, name=f"xw{o}") for o in range(PASSES)]
+        xs = keep.tile([P, T], U8, name="xs")
+        raw1 = [keep.tile([P, PACK, H], F32, name=f"raw1_{o}") for o in range(PASSES)]
+        raw2 = [keep.tile([P, PACK, H], F32, name=f"raw2_{o}", tag=f"raw2_{o}") for o in range(PASSES)]
+        raw3 = keep.tile([P, PACK, N], F32, name="raw3")
+
+        def rows(w, o):
+            return w[o * K_PASS : (o + 1) * K_PASS, :].rearrange("(p j) c -> p j c", j=PACK)
+
+        nc.gpsimd.memset(xs[:].bitcast(I32), 0)
+        nc.sync.dma_start(xw[0][:].bitcast(I32), x_words[0].rearrange("p c r -> p (c r)").bitcast(I32))
+        nc.sync.dma_start(offs_t[:], offs)
+        for q in range(4):
+            nc.sync.dma_start(
+                xs[32 * q : 32 * q + 4 * PASSES, :].bitcast(I32), x_scales[:, 4 * q : 4 * q + 4, :].bitcast(I32)
+            )
+        nc.sync.dma_start(raw1[0][:], rows(w1, 0))
+        nc.sync.dma_start(xw[1][:].bitcast(I32), x_words[1].rearrange("p c r -> p (c r)").bitcast(I32))
+        nc.sync.dma_start(raw1[1][:], rows(w1, 1))
+        nc.sync.dma_start(unit_t[:], unit.rearrange("(p t) one -> p (t one)", t=PACK))
+        nc.sync.dma_start(dn_t[:], dn)
+        nc.sync.dma_start(up_t[:], up_)
+        for o in range(PASSES):
+            nc.sync.dma_start(raw2[o][:], rows(w2, o))
+        nc.sync.dma_start(raw3[:], rows(w3, 0))
+
+        y = [keep.tile([P, Y_WIDTH], F32, name=f"y{t}") for t in range(PACK)]
+        z = [keep.tile([P, S + SPARE], F32, name=f"z{t}") for t in range(PACK)]
+        for win in y + z:
+            nc.vector.memset(win[:, S:], 0.0)
+
+        xq = [keep.tile([P, S], U32, name=f"xq{o}", align_bytes=64) for o in range(PASSES)]
+        xqs = keep.tile([P, S], U8, name="xqs", align_bytes=64)
+        nc.vector.tensor_copy(xq[0][:], xw[0][:].indirect(offs_t[:]))
+        nc.vector.tensor_copy(xqs[:], xs[:].indirect(offs_t[:]))
+
+        def deal(raw, name, split):
+            dealt = keep.tile([P, PACK * H], BF16, name=name, align_bytes=64)
+            dst = dealt[:].rearrange("p (t m j) -> p m j t", t=PACK, j=PACK)
+            src = raw[:].rearrange("p j (m t) -> p m j t", t=PACK)
+            nc.vector.tensor_copy(dst[:, :split], src[:, :split])
+            if split < P:
+                nc.scalar.copy(dst[:, split:].rearrange("p m j t -> p m t j"), src[:, split:].rearrange("p m j t -> p m t j"))
+            return dealt
+
+        def quantise(dealt, name, pieces):
+            words = dealt.shape[1] // PACK
+            codes = keep.tile([P, words], U32, name=name + "_codes", align_bytes=64)
+            scales = keep.tile([P, words], U8, name=name + "_scales", align_bytes=64)
+            step = words // pieces
+            for a in range(0, words, step):
+                nc.vector.quantize_mx(
+                    codes[:, a : a + step].bitcast(FP8X4), scales[:, a : a + step], dealt[:, PACK * a : PACK * (a + step)]
+                )
+            return codes, scales
+
+        def product(bank, wq, t, o):
+            cols = slice(t * P, (t + 1) * P)
+            nc.tensor.matmul_mx(
+                bank[:],
+                lhsT=wq[0][:, cols].bitcast(FP8X4),
+                lhsT_scale=wq[1][:, cols],
+                rhs=xq[o][:].bitcast(FP8X4),
+                rhs_scale=xqs[4 * o :, :],
+                start=(o == 0),
+                stop=(o == PASSES - 1),
+            )
+
+        y_banks = [psum.tile([P, S], F32, name=f"y_bank{t}", tag=f"bank{t}") for t in range(PACK)]
+        z_banks = [psum.tile([P, S], F32, name=f"z_bank{t}", tag=f"bank{PACK + t}") for t in range(PACK)]
+
+        w1q0 = quantise(deal(raw1[0], "dealt1_0", 48), "w1q0", 1)
+        nc.vector.tensor_copy(xq[1][:], xw[1][:].indirect(offs_t[:]))
+        for t in range(PACK):
+            product(y_banks[t], w1q0, t, 0)
+        w1q1 = quantise(deal(raw1[1], "dealt1_1", 88), "w1q1", 4)
+        for t in range(PACK):
+            product(y_banks[t], w1q1, t, 1)
+            if t < 2:
+                nc.scalar.activation(y[t][:, :S], y_banks[t][:], ACT.Copy, scale=unit_t[:, t : t + 1])
+            else:
+                nc.vector.tensor_scalar(y[t][:, :S], y_banks[t][:], unit_t[:, t : t + 1], None, ALU.mult)
+
+        for o in range(PASSES):
+            w2q = quantise(deal(raw2[o], f"dealt2_{o}", P), f"w2q{o}", 1)
+            for t in range(PACK):
+                product(z_banks[t], w2q, t, o)
+        for t in range(PACK):
+            nc.scalar.activation(z[t][:, :S], z_banks[t][:], ACT.Abs)
+
+        dealt3 = keep.tile([P, PACK * N], BF16, name="dealt3", align_bytes=64)
+        nc.scalar.copy(
+            dealt3[:].rearrange("p (c i j) -> p c j i", i=4, j=PACK), raw3[:].rearrange("p j (c i) -> p c j i", i=4)
+        )
+        w3q = quantise(dealt3, "w3q", 1)
+
+        def entries(r0, n):
+            return slice(r0 // STRIPE, (r0 + n) // STRIPE)
+
+        down = keep.tile([P, PACK, U], F32, name="down")
+        head = keep.tile([P, PACK, U], F32, name="head", tag="raw2_1")
+        for t in range(PACK):
+            nc.scalar.activation(down[:, t, :], y[t][:].indirect(dn_t[:]), ACT.Copy, scale=-1.0)
+            nc.vector.tensor_tensor(head[:, t, :], y[t][:].indirect(up_t[:]), down[:, t, :], ALU.add)
+
+        for c, n in enumerate(CHUNKS):
+            r0 = sum(CHUNKS[:c])
+            opening = keep.tile([P, PACK, n], F32, name=f"opening{c}")
+            for t in range(PACK):
+                nc.scalar.activation(opening[:, t, :], z[t][:].indirect(up_t[:, entries(r0, n)]), ACT.Copy)
+            hid = keep.tile([P, PACK * n], BF16, name=f"hid{c}", align_bytes=64)
+            nc.vector.tensor_tensor(
+                hid[:].rearrange("p (c i t) -> p c t i", i=4, t=PACK),
+                head[:, :, r0 : r0 + n].rearrange("p t (c i) -> p c t i", i=4),
+                opening[:].rearrange("p t (c i) -> p c t i", i=4),
+                ALU.mult,
+            )
+            hq = quantise(hid, f"hq{c}", 1)
+            bank = psum.tile([P, n], F32, name=f"gauge_bank{c}", tag=f"bank{c}")
+            nc.tensor.matmul_mx(
+                bank[:],
+                lhsT=w3q[0][:].bitcast(FP8X4),
+                lhsT_scale=w3q[1][:],
+                rhs=hq[0][:].bitcast(FP8X4),
+                rhs_scale=hq[1][:],
+                start=True,
+                stop=True,
+            )
+            result = keep.tile([P, n], F32, name=f"result{c}")
+            nc.scalar.copy(result[:], bank[:])
+            nc.sync.dma_start(out[:, r0 : r0 + n], result[:])

@@ -22,7 +22,7 @@ PASSES = K // K_PASS
 STRIPE = 16
 SPARE = 16
 Y_WIDTH = U + SPARE
-CHUNKS = (512, 256, 128, 128)
+CHUNKS = (384, 384, 128, 128)
 
 
 def tile_picked_yflowsq_lin_p_kernel(
@@ -39,7 +39,8 @@ def tile_picked_yflowsq_lin_p_kernel(
         unit_t = keep.tile([P, PACK], F32, name="unit_t")
         xw = [keep.tile([P, T], U32, name=f"xw{o}") for o in range(PASSES)]
         xs = keep.tile([P, T], U8, name="xs")
-        raw1 = [keep.tile([P, PACK, H], F32, name=f"raw1_{o}") for o in range(PASSES)]
+        raw1 = keep.tile([P, PACK, H], F32, name="raw1")
+        raw1_halves = [keep.tile([P, PACK, H // 2], F32, name=f"raw1_half{h}") for h in range(2)]
         raw2 = [keep.tile([P, PACK, H], F32, name=f"raw2_{o}", tag=f"raw2_{o}") for o in range(PASSES)]
         raw3 = keep.tile([P, PACK, N], F32, name="raw3")
 
@@ -53,34 +54,34 @@ def tile_picked_yflowsq_lin_p_kernel(
             nc.sync.dma_start(
                 xs[32 * q : 32 * q + 4 * PASSES, :].bitcast(I32), x_scales[:, 4 * q : 4 * q + 4, :].bitcast(I32)
             )
-        nc.sync.dma_start(raw1[0][:], rows(w1, 0))
+        nc.sync.dma_start(raw1[:], rows(w1, 0))
         nc.sync.dma_start(xw[1][:].bitcast(I32), x_words[1].rearrange("p c r -> p (c r)").bitcast(I32))
-        nc.sync.dma_start(raw1[1][:], rows(w1, 1))
+        for h in range(2):
+            nc.sync.dma_start(raw1_halves[h][:], rows(w1, 1)[:, :, h * H // 2 : (h + 1) * H // 2])
+        nc.sync.dma_start(raw3[:], rows(w3, 0))
         nc.sync.dma_start(unit_t[:], unit.rearrange("(p t) one -> p (t one)", t=PACK))
         nc.sync.dma_start(dn_t[:], dn)
         nc.sync.dma_start(up_t[:], up_)
         for o in range(PASSES):
             nc.sync.dma_start(raw2[o][:], rows(w2, o))
-        nc.sync.dma_start(raw3[:], rows(w3, 0))
 
         y = [keep.tile([P, Y_WIDTH], F32, name=f"y{t}") for t in range(PACK)]
-        z = [keep.tile([P, S + SPARE], F32, name=f"z{t}") for t in range(PACK)]
-        for win in y + z:
+        z = [keep.tile([P, S], F32, name=f"z{t}") for t in range(PACK)]
+        for win in y:
             nc.vector.memset(win[:, S:], 0.0)
 
-        xq = [keep.tile([P, S], U32, name=f"xq{o}", align_bytes=64) for o in range(PASSES)]
+        xq = [keep.tile([P, S], U32, name="xq0", align_bytes=64)]
         xqs = keep.tile([P, S], U8, name="xqs", align_bytes=64)
         nc.vector.tensor_copy(xq[0][:], xw[0][:].indirect(offs_t[:]))
         nc.vector.tensor_copy(xqs[:], xs[:].indirect(offs_t[:]))
 
-        def deal(raw, name, split):
-            dealt = keep.tile([P, PACK * H], BF16, name=name, align_bytes=64)
+        def deal(copy, dealt, raw, m0, m1, first=0):
             dst = dealt[:].rearrange("p (t m j) -> p m j t", t=PACK, j=PACK)
             src = raw[:].rearrange("p j (m t) -> p m j t", t=PACK)
-            nc.vector.tensor_copy(dst[:, :split], src[:, :split])
-            if split < P:
-                nc.scalar.copy(dst[:, split:].rearrange("p m j t -> p m t j"), src[:, split:].rearrange("p m j t -> p m t j"))
-            return dealt
+            copy(dst[:, m0:m1], src[:, m0 - first : m1 - first])
+
+        def dealt_tile(name):
+            return keep.tile([P, PACK * H], BF16, name=name, tag=name, align_bytes=64)
 
         def quantise(dealt, name, pieces):
             words = dealt.shape[1] // PACK
@@ -93,45 +94,56 @@ def tile_picked_yflowsq_lin_p_kernel(
                 )
             return codes, scales
 
-        def product(bank, wq, t, o):
+        def product(bank, wq, t, o, j0=0, j1=S):
             cols = slice(t * P, (t + 1) * P)
             nc.tensor.matmul_mx(
                 bank[:],
                 lhsT=wq[0][:, cols].bitcast(FP8X4),
                 lhsT_scale=wq[1][:, cols],
-                rhs=xq[o][:].bitcast(FP8X4),
-                rhs_scale=xqs[4 * o :, :],
+                rhs=xq[o][:, j0:j1].bitcast(FP8X4),
+                rhs_scale=xqs[4 * o :, j0:j1],
                 start=(o == 0),
                 stop=(o == PASSES - 1),
             )
 
-        y_banks = [psum.tile([P, S], F32, name=f"y_bank{t}", tag=f"bank{t}") for t in range(PACK)]
-        z_banks = [psum.tile([P, S], F32, name=f"z_bank{t}", tag=f"bank{PACK + t}") for t in range(PACK)]
+        y_parts = [(0, 0, S // 2, 0), (0, S // 2, S, 2 * PACK - 1)] + [(t, 0, S, t) for t in range(1, PACK)]
+        y_banks = [psum.tile([P, j1 - j0], F32, name=f"y_bank{b}", tag=f"bank{b}") for t, j0, j1, b in y_parts]
 
-        w1q0 = quantise(deal(raw1[0], "dealt1_0", 48), "w1q0", 1)
+        dealt = dealt_tile("dealt1_0")
+        deal(nc.vector.tensor_copy, dealt, raw1, 0, 80)
+        deal(nc.scalar.copy, dealt, raw1, 80, P)
+        w1q0 = quantise(dealt, "w1q0", 2)
+        xq.append(keep.tile([P, S], U32, name="xq1", tag="dealt1_0", align_bytes=64))
         nc.vector.tensor_copy(xq[1][:], xw[1][:].indirect(offs_t[:]))
-        for t in range(PACK):
-            product(y_banks[t], w1q0, t, 0)
-        w1q1 = quantise(deal(raw1[1], "dealt1_1", 88), "w1q1", 4)
-        for t in range(PACK):
-            product(y_banks[t], w1q1, t, 1)
-            if t < 2:
-                nc.scalar.activation(y[t][:, :S], y_banks[t][:], ACT.Copy, scale=unit_t[:, t : t + 1])
-            else:
-                nc.vector.tensor_scalar(y[t][:, :S], y_banks[t][:], unit_t[:, t : t + 1], None, ALU.mult)
-
-        for o in range(PASSES):
-            w2q = quantise(deal(raw2[o], f"dealt2_{o}", P), f"w2q{o}", 1)
-            for t in range(PACK):
-                product(z_banks[t], w2q, t, o)
-        for t in range(PACK):
-            nc.scalar.activation(z[t][:, :S], z_banks[t][:], ACT.Abs)
-
+        for bank, (t, j0, j1, b) in zip(y_banks, y_parts):
+            product(bank, w1q0, t, 0, j0, j1)
+        dealt = dealt_tile("dealt1_1")
+        deal(nc.scalar.copy, dealt, raw1_halves[0], 0, 64)
+        deal(nc.vector.tensor_copy, dealt, raw1_halves[1], 64, 108, 64)
+        deal(nc.scalar.copy, dealt, raw1_halves[1], 108, P, 64)
+        w1q1 = quantise(dealt, "w1q1", 4)
         dealt3 = keep.tile([P, PACK * N], BF16, name="dealt3", align_bytes=64)
         nc.scalar.copy(
             dealt3[:].rearrange("p (c i j) -> p c j i", i=4, j=PACK), raw3[:].rearrange("p j (c i) -> p c j i", i=4)
         )
         w3q = quantise(dealt3, "w3q", 1)
+
+        for bank, (t, j0, j1, b) in zip(y_banks, y_parts):
+            product(bank, w1q1, t, 1, j0, j1)
+            if j0 > 0:
+                nc.scalar.activation(y[t][:, j0:j1], bank[:], ACT.Copy, scale=unit_t[:, t : t + 1])
+            else:
+                nc.vector.tensor_scalar(y[t][:, j0:j1], bank[:], unit_t[:, t : t + 1], None, ALU.mult)
+
+        z_banks = [psum.tile([P, S], F32, name=f"z_bank{t}", tag=f"bank{PACK + t}") for t in range(PACK)]
+        for o in range(PASSES):
+            dealt = dealt_tile(f"dealt2_{o}")
+            deal(nc.vector.tensor_copy, dealt, raw2[o], 0, P)
+            w2q = quantise(dealt, f"w2q{o}", 1)
+            for t in range(PACK):
+                product(z_banks[t], w2q, t, o)
+        for t in range(PACK):
+            nc.scalar.activation(z[t][:], z_banks[t][:], ACT.Abs)
 
         def entries(r0, n):
             return slice(r0 // STRIPE, (r0 + n) // STRIPE)
@@ -146,7 +158,11 @@ def tile_picked_yflowsq_lin_p_kernel(
             r0 = sum(CHUNKS[:c])
             opening = keep.tile([P, PACK, n], F32, name=f"opening{c}")
             for t in range(PACK):
-                nc.scalar.activation(opening[:, t, :], z[t][:].indirect(up_t[:, entries(r0, n)]), ACT.Copy)
+                picked = z[t][:].indirect(up_t[:, entries(r0, n)])
+                if c == 1 and t == PACK - 1:
+                    nc.vector.tensor_copy(opening[:, t, :], picked)
+                else:
+                    nc.scalar.activation(opening[:, t, :], picked, ACT.Copy)
             hid = keep.tile([P, PACK * n], BF16, name=f"hid{c}", align_bytes=64)
             nc.vector.tensor_tensor(
                 hid[:].rearrange("p (c i t) -> p c t i", i=4, t=PACK),
@@ -156,15 +172,17 @@ def tile_picked_yflowsq_lin_p_kernel(
             )
             hq = quantise(hid, f"hq{c}", 1)
             bank = psum.tile([P, n], F32, name=f"gauge_bank{c}", tag=f"bank{c}")
-            nc.tensor.matmul_mx(
-                bank[:],
-                lhsT=w3q[0][:].bitcast(FP8X4),
-                lhsT_scale=w3q[1][:],
-                rhs=hq[0][:].bitcast(FP8X4),
-                rhs_scale=hq[1][:],
-                start=True,
-                stop=True,
-            )
+            for a in range(0, n, 256):
+                cols = slice(a, min(a + 256, n))
+                nc.tensor.matmul_mx(
+                    bank[:, cols],
+                    lhsT=w3q[0][:].bitcast(FP8X4),
+                    lhsT_scale=w3q[1][:],
+                    rhs=hq[0][:, cols].bitcast(FP8X4),
+                    rhs_scale=hq[1][:, cols],
+                    start=True,
+                    stop=True,
+                )
             result = keep.tile([P, n], F32, name=f"result{c}")
             nc.scalar.copy(result[:], bank[:])
             nc.sync.dma_start(out[:, r0 : r0 + n], result[:])

from contextlib import ExitStack

import concourse.mybir as mybir

K, T, S, N, H, U = 1024, 1024, 512, 128, 512, 1024
FLOPS = 2 * (2 * K * H * S + H * N * U)

F32 = mybir.dt.float32
BF16 = mybir.dt.bfloat16
I32 = mybir.dt.int32
U32 = mybir.dt.uint32
U16 = mybir.dt.uint16
U8 = mybir.dt.uint8
FP8X4 = mybir.dt.float8_e4m3fn_x4
ALU = mybir.AluOpType
ACT = mybir.ActivationFunctionType

P = 128
PACK = 4
K_PASS = P * PACK
PASSES = K // K_PASS
STRIPE = 16
SPARE = 16
Y_WIDTH = U + SPARE
CHUNKS = (384, 384, 128, 128)


def tile_picked_yflowsq_lin_p_kernel(
    tc, x_words, x_scales, w1, w2, unit, w3, offs, up_, dn, out
):
    nc = tc.nc
    with ExitStack() as ctx:
        keep = ctx.enter_context(tc.tile_pool(name="keep", bufs=1))
        psum = ctx.enter_context(tc.psum_pool(name="psum", bufs=1))

        offs_t = keep.tile([P, S // STRIPE], U16, name="offs_t")
        up_t = keep.tile([P, U // STRIPE], U16, name="up_t")
        dn_t = keep.tile([P, U // STRIPE], U16, name="dn_t")
        unit_t = keep.tile([P, PACK], F32, name="unit_t")
        xw = [keep.tile([P, T], U32, name=f"xw{o}") for o in range(PASSES)]
        xs = keep.tile([P, T], U8, name="xs")
        raw1 = keep.tile([P, PACK, H], F32, name="raw1")
        raw1_halves = [keep.tile([P, PACK, H // 2], F32, name=f"raw1_half{h}") for h in range(2)]
        raw2 = [keep.tile([P, PACK, H], F32, name=f"raw2_{o}", tag=f"raw2_{o}") for o in range(PASSES)]
        raw3 = keep.tile([P, PACK, N], F32, name="raw3")

        def rows(w, o):
            return w[o * K_PASS : (o + 1) * K_PASS, :].rearrange("(p j) c -> p j c", j=PACK)

        nc.gpsimd.memset(xs[:].bitcast(I32), 0)
        nc.sync.dma_start(xw[0][:].bitcast(I32), x_words[0].rearrange("p c r -> p (c r)").bitcast(I32))
        nc.sync.dma_start(offs_t[:], offs)
        for q in range(4):
            nc.sync.dma_start(
                xs[32 * q : 32 * q + 4 * PASSES, :].bitcast(I32), x_scales[:, 4 * q : 4 * q + 4, :].bitcast(I32)
            )
        nc.sync.dma_start(raw1[:], rows(w1, 0))
        nc.sync.dma_start(xw[1][:].bitcast(I32), x_words[1].rearrange("p c r -> p (c r)").bitcast(I32))
        for h in range(2):
            nc.sync.dma_start(raw1_halves[h][:], rows(w1, 1)[:, :, h * H // 2 : (h + 1) * H // 2])
        nc.sync.dma_start(raw3[:], rows(w3, 0))
        nc.sync.dma_start(unit_t[:], unit.rearrange("(p t) one -> p (t one)", t=PACK))
        nc.sync.dma_start(dn_t[:], dn)
        nc.sync.dma_start(up_t[:], up_)
        for o in range(PASSES):
            nc.sync.dma_start(raw2[o][:], rows(w2, o))

        y = [keep.tile([P, Y_WIDTH], F32, name=f"y{t}") for t in range(PACK)]
        z = [keep.tile([P, S], F32, name=f"z{t}") for t in range(PACK)]
        for win in y:
            nc.vector.memset(win[:, S:], 0.0)

        xq = [keep.tile([P, S], U32, name="xq0", align_bytes=64)]
        xqs = keep.tile([P, S], U8, name="xqs", align_bytes=64)
        nc.vector.tensor_copy(xq[0][:], xw[0][:].indirect(offs_t[:]))
        nc.vector.tensor_copy(xqs[:], xs[:].indirect(offs_t[:]))

        def deal(copy, dealt, raw, m0, m1, first=0):
            dst = dealt[:].rearrange("p (t m j) -> p m j t", t=PACK, j=PACK)
            src = raw[:].rearrange("p j (m t) -> p m j t", t=PACK)
            copy(dst[:, m0:m1], src[:, m0 - first : m1 - first])

        def dealt_tile(name):
            return keep.tile([P, PACK * H], BF16, name=name, tag=name, align_bytes=64)

        def quantise(dealt, name, pieces):
            words = dealt.shape[1] // PACK
            codes = keep.tile([P, words], U32, name=name + "_codes", align_bytes=64)
            scales = keep.tile([P, words], U8, name=name + "_scales", align_bytes=64)
            step = words // pieces
            for a in range(0, words, step):
                nc.vector.quantize_mx(
                    codes[:, a : a + step].bitcast(FP8X4), scales[:, a : a + step], dealt[:, PACK * a : PACK * (a + step)]
                )
            return codes, scales

        def product(bank, wq, t, o, j0=0, j1=S):
            cols = slice(t * P, (t + 1) * P)
            nc.tensor.matmul_mx(
                bank[:],
                lhsT=wq[0][:, cols].bitcast(FP8X4),
                lhsT_scale=wq[1][:, cols],
                rhs=xq[o][:, j0:j1].bitcast(FP8X4),
                rhs_scale=xqs[4 * o :, j0:j1],
                start=(o == 0),
                stop=(o == PASSES - 1),
            )

        y_parts = [(0, 0, S // 2, 0), (0, S // 2, S, 2 * PACK - 1)] + [(t, 0, S, t) for t in range(1, PACK)]
        y_banks = [psum.tile([P, j1 - j0], F32, name=f"y_bank{b}", tag=f"bank{b}") for t, j0, j1, b in y_parts]

        dealt = dealt_tile("dealt1_0")
        deal(nc.vector.tensor_copy, dealt, raw1, 0, 80)
        deal(nc.scalar.copy, dealt, raw1, 80, P)
        w1q0 = quantise(dealt, "w1q0", 2)
        xq.append(keep.tile([P, S], U32, name="xq1", tag="dealt1_0", align_bytes=64))
        nc.vector.tensor_copy(xq[1][:], xw[1][:].indirect(offs_t[:]))
        for bank, (t, j0, j1, b) in zip(y_banks, y_parts):
            product(bank, w1q0, t, 0, j0, j1)
        dealt = dealt_tile("dealt1_1")
        deal(nc.scalar.copy, dealt, raw1_halves[0], 0, 64)
        deal(nc.vector.tensor_copy, dealt, raw1_halves[1], 64, 108, 64)
        deal(nc.scalar.copy, dealt, raw1_halves[1], 108, P, 64)
        w1q1 = quantise(dealt, "w1q1", 4)
        dealt3 = keep.tile([P, PACK * N], BF16, name="dealt3", align_bytes=64)
        nc.scalar.copy(
            dealt3[:].rearrange("p (c i j) -> p c j i", i=4, j=PACK), raw3[:].rearrange("p j (c i) -> p c j i", i=4)
        )
        w3q = quantise(dealt3, "w3q", 1)

        for bank, (t, j0, j1, b) in zip(y_banks, y_parts):
            product(bank, w1q1, t, 1, j0, j1)
            if j0 > 0:
                nc.scalar.activation(y[t][:, j0:j1], bank[:], ACT.Copy, scale=unit_t[:, t : t + 1])
            else:
                nc.vector.tensor_scalar(y[t][:, j0:j1], bank[:], unit_t[:, t : t + 1], None, ALU.mult)

        z_banks = [psum.tile([P, S], F32, name=f"z_bank{t}", tag=f"bank{PACK + t}") for t in range(PACK)]
        for o in range(PASSES):
            dealt = dealt_tile(f"dealt2_{o}")
            deal(nc.vector.tensor_copy, dealt, raw2[o], 0, P)
            w2q = quantise(dealt, f"w2q{o}", 1)
            for t in range(PACK):
                product(z_banks[t], w2q, t, o)
        for t in range(PACK):
            nc.scalar.activation(z[t][:], z_banks[t][:], ACT.Abs)

        def entries(r0, n):
            return slice(r0 // STRIPE, (r0 + n) // STRIPE)

        down = keep.tile([P, PACK, U], F32, name="down")
        head = keep.tile([P, PACK, U], F32, name="head", tag="raw2_1")
        for t in range(PACK):
            nc.scalar.activation(down[:, t, :], y[t][:].indirect(dn_t[:]), ACT.Copy, scale=-1.0)
            nc.vector.tensor_tensor(head[:, t, :], y[t][:].indirect(up_t[:]), down[:, t, :], ALU.add)

        for c, n in enumerate(CHUNKS):
            r0 = sum(CHUNKS[:c])
            opening = keep.tile([P, PACK, n], F32, name=f"opening{c}")
            for t in range(PACK):
                picked = z[t][:].indirect(up_t[:, entries(r0, n)])
                if c == 1 and t == PACK - 1:
                    nc.vector.tensor_copy(opening[:, t, :], picked)
                else:
                    nc.scalar.activation(opening[:, t, :], picked, ACT.Copy)
            hid = keep.tile([P, PACK * n], BF16, name=f"hid{c}", align_bytes=64)
            nc.vector.tensor_tensor(
                hid[:].rearrange("p (c i t) -> p c t i", i=4, t=PACK),
                head[:, :, r0 : r0 + n].rearrange("p t (c i) -> p c t i", i=4),
                opening[:].rearrange("p t (c i) -> p c t i", i=4),
                ALU.mult,
            )
            hq = quantise(hid, f"hq{c}", 1)
            bank = psum.tile([P, n], F32, name=f"gauge_bank{c}", tag=f"bank{c}")
            for a in range(0, n, 256):
                cols = slice(a, min(a + 256, n))
                nc.tensor.matmul_mx(
                    bank[:, cols],
                    lhsT=w3q[0][:].bitcast(FP8X4),
                    lhsT_scale=w3q[1][:],
                    rhs=hq[0][:, cols].bitcast(FP8X4),
                    rhs_scale=hq[1][:, cols],
                    start=True,
                    stop=True,
                )
            result = keep.tile([P, n], F32, name=f"result{c}")
            nc.scalar.copy(result[:], bank[:])
            nc.sync.dma_start(out[:, r0 : r0 + n], result[:])
